import numpy as np
import ml_dtypes


def mxq(x, axis, fmt="e4m3"):
    dtype, down = {"e4m3": (ml_dtypes.float8_e4m3fn, 7), "e5m2": (ml_dtypes.float8_e5m2, 14)}[fmt]
    v = np.moveaxis(np.asarray(x, np.float32).astype(ml_dtypes.bfloat16).astype(np.float64), axis, -1)
    blocks = v.reshape(v.shape[:-1] + (-1, 32))
    amax = np.abs(blocks).max(-1, keepdims=True)
    byte = np.maximum(np.where(amax > 0, np.frexp(amax)[1] - 1 + 127, 0) - down, 1)
    scale = np.exp2(byte - 127.0)
    codes = (blocks / scale).astype(np.float32).astype(dtype).astype(np.float64)
    return np.moveaxis((codes * scale).reshape(v.shape), -1, axis)


WIDE = False


def mx_kscale(k, group=512):
    if not WIDE:
        return np.ones(k)
    levels = np.array([18, -18])
    if group != 512:
        return np.exp2(np.random.permutation(np.resize(levels, k // group))).repeat(group)
    if k % 512:
        return np.exp2(np.random.permutation(np.resize(levels, k // 32))).repeat(32)
    a = np.empty((k // 512, 16))
    for p in range(k // 512):
        a[p, :8] = np.random.permutation(np.resize(levels, 8))
        for g in range(8):
            far = levels[np.abs(levels - a[p, g]) >= 10]
            a[p, g + 8] = far[np.random.randint(len(far))]
    return np.exp2(a.ravel()).repeat(32)


def f64(x):
    return np.asarray(x).astype(np.float64)


G, D, M, O, N = 4, 128, 128, 128, 512


def sgn(shape):
    return np.random.uniform(0.5, 2.0, shape) * np.where(np.random.standard_normal(shape) < 0, -1.0, 1.0)


def setup_inputs():
    n = np.random.standard_normal
    s_d = mx_kscale(D, 0)
    s_m = mx_kscale(M, 0)
    return {
        "x": (n((G, D, N)) * s_d[:, None]).astype(np.float32),
        "w1": (n((G, D, M)) / np.sqrt(D) / s_d[:, None]).astype(np.float32),
        "w2": (n((G, D, M)) / np.sqrt(D) / s_d[:, None]).astype(np.float32),
        "w3": (n((G, D, M)) / np.sqrt(D) / s_d[:, None]).astype(np.float32),
        "hs": (sgn((G, M, 1)) * s_m[:, None]).astype(np.float32),
        "wo2": (n((G, M, O)) / np.sqrt(M) / s_m[:, None]).astype(np.float32),
        "res": (0.5 * n((G, O, N))).astype(np.float32),
    }


def reference(x, w1, w2, w3, hs, wo2, res):
    w1q = mxq(f64(w1), 1, "e4m3")
    xq = mxq(f64(x), 1, "e4m3")
    z1 = w1q.transpose(0, 2, 1) @ xq
    w2q = mxq(f64(w2), 1, "e4m3")
    z2 = w2q.transpose(0, 2, 1) @ xq
    w3q = mxq(f64(w3), 1, "e4m3")
    z3 = w3q.transpose(0, 2, 1) @ xq
    se = np.exp(z1) + np.exp(z2) + np.exp(z3)
    h = np.log(se) * np.tanh(z1)
    hh = h * f64(hs)
    wo2q = mxq(f64(wo2), 1, "e4m3")
    hhq = mxq(hh, 1, "e4m3")
    y0 = wo2q.transpose(0, 2, 1) @ hhq
    y = y0 + f64(res)
    return y

@@ -1,0 +1,176 @@
+from contextlib import ExitStack
+
+import concourse.mybir as mybir
+
+G, D, M, O, N = 4, 128, 128, 128, 512
+FLOPS = 2 * G * D * M * N * 3 + 2 * G * M * O * N
+
+F32 = mybir.dt.float32
+BF16 = mybir.dt.bfloat16
+U32 = mybir.dt.uint32
+U8 = mybir.dt.uint8
+FP8X4 = mybir.dt.float8_e4m3fn_x4
+ACT = mybir.ActivationFunctionType
+ALU = mybir.AluOpType
+
+P = 128
+PACK = 4
+ROWS = 32
+CW = 128
+CHUNKS = N // CW
+RUN = 4
+
+
+def tile_rows_fsoftmaxthree_kernel(tc, x, w1, w2, w3, hs, wo2, res, out):
+    nc = tc.nc
+    with ExitStack() as ctx:
+        sb = ctx.enter_context(tc.tile_pool(name="sb", bufs=1))
+        ps = ctx.enter_context(tc.psum_pool(name="ps", bufs=1))
+        ctx.enter_context(tc.manual_schedule())
+
+        banks = [[ps.tile([P, 512], F32, name="bank%d_%d" % (g, s)) for s in range(2)] for g in range(G)]
+
+        def load_packed(name, src):
+            raw = sb.tile([P, PACK, CW], F32, name=name + "_raw")
+            nc.sync.dma_start(out=raw[:], in_=src)
+            return raw
+
+        def interleave(name, raw, on_scalar):
+            grouped = sb.tile([P, CW * PACK], BF16, name=name + "_grp", align_bytes=64)
+            dst = grouped[:].rearrange("p (c i t) -> p c t i", i=RUN, t=PACK)
+            src = raw[:].rearrange("p t (c i) -> p c t i", i=RUN)
+            if on_scalar:
+                nc.scalar.activation(out=dst, in_=src, func=ACT.Copy)
+            else:
+                nc.vector.tensor_copy(out=dst, in_=src)
+            return grouped
+
+        def quantize(name, grouped):
+            codes = sb.tile([P, CW], U32, name=name + "_codes", align_bytes=64)
+            scales = sb.tile([P, CW], U8, name=name + "_scales", align_bytes=64)
+            nc.vector.quantize_mx(out=codes[:].bitcast(FP8X4), scales=scales[:], in_=grouped[:])
+            return codes, scales
+
+        def product(dst, g, stationary, moving):
+            rows = slice(ROWS * g, ROWS * (g + 1))
+            nc.tensor.matmul_mx(
+                out=dst,
+                lhsT=stationary[0][rows, :].bitcast(FP8X4),
+                lhsT_scale=stationary[1][rows, :],
+                rhs=moving[0][rows, :].bitcast(FP8X4),
+                rhs_scale=moving[1][rows, :],
+                start=True,
+                stop=True,
+            )
+
+        def packed_view(a):
+            return a.rearrange("g (p j) c -> (g p) j c", j=PACK)
+
+        xv = packed_view(x)
+        w1_raw = load_packed("w1", packed_view(w1))
+        x_raw = [load_packed("x0", xv[:, :, 0:CW])]
+        w2_raw = load_packed("w2", packed_view(w2))
+        w3_raw = load_packed("w3", packed_view(w3))
+        for c in range(1, CHUNKS):
+            x_raw.append(load_packed("x%d" % c, xv[:, :, c * CW : (c + 1) * CW]))
+        wo_raw = load_packed("wo", packed_view(wo2))
+        hs_sb = sb.tile([P, G], F32, name="hs_sb")
+        with nc.allow_non_contiguous_dma(reason="one scale for each partition and group"):
+            nc.sync.dma_start(out=hs_sb[:], in_=hs.rearrange("g m o -> m (g o)"))
+        res_sb = sb.tile([P, G, N], F32, name="res_sb")
+        nc.sync.dma_start(out=res_sb[:], in_=res.rearrange("g o n -> o g n"))
+
+        e = [sb.tile([P, G, 3 * CW], F32, name="e%d" % c) for c in range(CHUNKS)]
+        th = [sb.tile([P, G, CW], F32, name="th%d" % c) for c in range(CHUNKS)]
+        part = [sb.tile([P, G, CW], F32, name="part%d" % c) for c in range(CHUNKS)]
+        se = [sb.tile([P, G, CW], F32, name="se%d" % c) for c in range(CHUNKS)]
+
+        def add_first(c):
+            nc.vector.tensor_tensor(out=part[c][:], in0=e[c][:, :, 0:CW], in1=e[c][:, :, CW : 2 * CW], op=ALU.add)
+
+        def add_second(c):
+            nc.vector.tensor_tensor(out=se[c][:], in0=part[c][:], in1=e[c][:, :, 2 * CW : 3 * CW], op=ALU.add)
+
+        w1_g = interleave("w1", w1_raw, True)
+        x0_g = interleave("x0", x_raw[0], False)
+        w1_q = quantize("w1", w1_g)
+        x0_q = quantize("x0", x0_g)
+        w2_g = interleave("w2", w2_raw, True)
+        for g in range(G):
+            product(banks[g][0][:, 0:CW], g, w1_q, x0_q)
+        w3_g = interleave("w3", w3_raw, False)
+        w2_q = quantize("w2", w2_g)
+        w3_q = quantize("w3", w3_g)
+        w_q = [w1_q, w2_q, w3_q]
+        for b in (1, 2):
+            for g in range(G):
+                product(banks[g][1][:, (b - 1) * CW : b * CW], g, w_q[b], x0_q)
+        for g in range(G):
+            nc.scalar.activation(out=th[0][:, g, :], in_=banks[g][0][:, 0:CW], func=ACT.Tanh)
+            nc.scalar.activation(out=e[0][:, g, 0:CW], in_=banks[g][0][:, 0:CW], func=ACT.Exp)
+        for g in range(G):
+            nc.scalar.activation(out=e[0][:, g, CW : 3 * CW], in_=banks[g][1][:, 0 : 2 * CW], func=ACT.Exp)
+
+        def first_layer(c, x_q):
+            s = (c + 1) % 2
+            for b in range(3):
+                for g in range(G):
+                    product(banks[g][s][:, b * CW : (b + 1) * CW], g, w_q[b], x_q)
+            for g in range(G):
+                nc.scalar.activation(out=e[c][:, g, :], in_=banks[g][s][:, 0 : 3 * CW], func=ACT.Exp)
+                nc.scalar.activation(out=th[c][:, g, :], in_=banks[g][s][:, 0:CW], func=ACT.Tanh)
+
+        x1_g = interleave("x1", x_raw[1], False)
+        x1_q = quantize("x1", x1_g)
+        first_layer(1, x1_q)
+        x2_g = interleave("x2", x_raw[2], False)
+        x3_g = interleave("x3", x_raw[3], False)
+        x2_q = quantize("x2", x2_g)
+        x3_q = quantize("x3", x3_g)
+        add_first(0)
+        wo_g = interleave("wo", wo_raw, False)
+        add_second(0)
+        wo_q = quantize("wo", wo_g)
+        first_layer(2, x2_q)
+        add_first(1)
+        add_second(1)
+        first_layer(3, x3_q)
+        for c in (2, 3):
+            add_first(c)
+            add_second(c)
+
+        lse = [sb.tile([P, G, CW], F32, name="lse%d" % c) for c in range(CHUNKS)]
+        hh = [sb.tile([P, G, CW], BF16, name="hh%d" % c) for c in range(CHUNKS)]
+        moved = [sb.tile([P, PACK, CW], BF16, name="moved%d" % c) for c in range(CHUNKS)]
+        for c in range(CHUNKS):
+            for half in range(2):
+                gs = slice(2 * half, 2 * half + 2)
+                nc.scalar.activation(out=lse[c][:, gs, :], in_=se[c][:, gs, :], func=ACT.Ln)
+            for g in range(G):
+                nc.vector.scalar_tensor_tensor(
+                    out=hh[c][:, g, :], in0=th[c][:, g, :], scalar=hs_sb[:, g : g + 1], in1=lse[c][:, g, :],
+                    op0=ALU.mult, op1=ALU.mult,
+                )
+                nc.sync.dma_start(out=moved[c][ROWS * g : ROWS * (g + 1), :, :], in_=hh[c][:, g, :])
+
+        outv = out.rearrange("g o n -> o g n")
+
+        def second_product(c):
+            hh_g = interleave("hh%d" % c, moved[c], True)
+            hh_q = quantize("hh%d" % c, hh_g)
+            for g in range(G):
+                product(banks[g][c % 2][:, 0:CW], g, wo_q, hh_q)
+
+        def finish(c):
+            cols = slice(c * CW, (c + 1) * CW)
+            y = sb.tile([P, G, CW], F32, name="y%d" % c)
+            for g in range(G):
+                nc.vector.tensor_tensor(out=y[:, g, :], in0=banks[g][c % 2][:, 0:CW], in1=res_sb[:, g, cols], op=ALU.add)
+                if g % 2 == 1:
+                    nc.sync.dma_start(out=outv[:, g - 1 : g + 1, cols], in_=y[:, g - 1 : g + 1, :])
+
+        second_product(0)
+        for c in range(CHUNKS):
+            if c + 1 < CHUNKS:
+                second_product(c + 1)
+            finish(c)

@@ -30,35 +30,40 @@ def tile_rows_fsoftmaxthree_kernel(tc, x, w1, w2, w3, hs, wo2, res, out):
 
         banks = [[ps.tile([P, 512], F32, name="bank%d_%d" % (g, s)) for s in range(2)] for g in range(G)]
 
-        def load_packed(name, src):
-            raw = sb.tile([P, PACK, CW], F32, name=name + "_raw")
+        def load_packed(name, src, width):
+            raw = sb.tile([P, PACK, width], F32, name=name + "_raw")
             nc.sync.dma_start(out=raw[:], in_=src)
             return raw
 
-        def interleave(name, raw, on_scalar):
-            grouped = sb.tile([P, CW * PACK], BF16, name=name + "_grp", align_bytes=64)
-            dst = grouped[:].rearrange("p (c i t) -> p c t i", i=RUN, t=PACK)
-            src = raw[:].rearrange("p t (c i) -> p c t i", i=RUN)
+        def word_order(flat, run=RUN):
+            return flat.rearrange("p (c i t) -> p c t i", i=run, t=PACK)
+
+        def row_order(rows, run=RUN):
+            return rows.rearrange("p t (c i) -> p c t i", i=run)
+
+        def interleave(name, raw, width, on_scalar):
+            grouped = sb.tile([P, width * PACK], BF16, name=name + "_grp", align_bytes=64)
             if on_scalar:
-                nc.scalar.activation(out=dst, in_=src, func=ACT.Copy)
+                nc.scalar.activation(out=word_order(grouped[:]), in_=row_order(raw[:]), func=ACT.Copy)
             else:
-                nc.vector.tensor_copy(out=dst, in_=src)
+                nc.vector.tensor_copy(out=word_order(grouped[:]), in_=row_order(raw[:]))
             return grouped
 
-        def quantize(name, grouped):
-            codes = sb.tile([P, CW], U32, name=name + "_codes", align_bytes=64)
-            scales = sb.tile([P, CW], U8, name=name + "_scales", align_bytes=64)
+        def quantize(name, grouped, width):
+            codes = sb.tile([P, width], U32, name=name + "_codes", align_bytes=64)
+            scales = sb.tile([P, width], U8, name=name + "_scales", align_bytes=64)
             nc.vector.quantize_mx(out=codes[:].bitcast(FP8X4), scales=scales[:], in_=grouped[:])
             return codes, scales
 
-        def product(dst, g, stationary, moving):
+        def product(dst, g, stationary, moving, col0):
             rows = slice(ROWS * g, ROWS * (g + 1))
+            cols = slice(col0, col0 + CW)
             nc.tensor.matmul_mx(
                 out=dst,
                 lhsT=stationary[0][rows, :].bitcast(FP8X4),
                 lhsT_scale=stationary[1][rows, :],
-                rhs=moving[0][rows, :].bitcast(FP8X4),
-                rhs_scale=moving[1][rows, :],
+                rhs=moving[0][rows, cols].bitcast(FP8X4),
+                rhs_scale=moving[1][rows, cols],
                 start=True,
                 stop=True,
             )
@@ -67,110 +72,167 @@ def tile_rows_fsoftmaxthree_kernel(tc, x, w1, w2, w3, hs, wo2, res, out):
             return a.rearrange("g (p j) c -> (g p) j c", j=PACK)
 
         xv = packed_view(x)
-        w1_raw = load_packed("w1", packed_view(w1))
-        x_raw = [load_packed("x0", xv[:, :, 0:CW])]
-        w2_raw = load_packed("w2", packed_view(w2))
-        w3_raw = load_packed("w3", packed_view(w3))
-        for c in range(1, CHUNKS):
-            x_raw.append(load_packed("x%d" % c, xv[:, :, c * CW : (c + 1) * CW]))
-        wo_raw = load_packed("wo", packed_view(wo2))
-        hs_sb = sb.tile([P, G], F32, name="hs_sb")
-        with nc.allow_non_contiguous_dma(reason="one scale for each partition and group"):
-            nc.sync.dma_start(out=hs_sb[:], in_=hs.rearrange("g m o -> m (g o)"))
+        hs_rows = sb.tile([P, ROWS], F32, name="hs_rows", align_bytes=64)
+        hs_cols = sb.tile([P, ROWS], F32, name="hs_cols", align_bytes=64)
+        nc.vector.memset(hs_rows[:], 0.0)
+        w1_raw = load_packed("w1", packed_view(w1), CW)
+        x0_raw = load_packed("x0", xv[:, :, 0:CW], CW)
+        w2_raw = load_packed("w2", packed_view(w2), CW)
+        w3_raw = load_packed("w3", packed_view(w3), CW)
+        x1_raw = load_packed("x1", xv[:, :, CW : 2 * CW], CW)
+        nc.sync.dma_start(out=hs_rows[0:P:8, :], in_=hs.rearrange("g (b c) o -> b g (c o)", c=ROWS))
+        xl_raw = load_packed("xl", xv[:, :, 2 * CW : 4 * CW], 2 * CW)
+        wo_raw = load_packed("wo", packed_view(wo2), CW)
         res_sb = sb.tile([P, G, N], F32, name="res_sb")
         nc.sync.dma_start(out=res_sb[:], in_=res.rearrange("g o n -> o g n"))
+
+        def scale_of(g):
+            return hs_cols[:, 8 * g : 8 * g + 1]
 
         e = [sb.tile([P, G, 3 * CW], F32, name="e%d" % c) for c in range(CHUNKS)]
         th = [sb.tile([P, G, CW], F32, name="th%d" % c) for c in range(CHUNKS)]
         part = [sb.tile([P, G, CW], F32, name="part%d" % c) for c in range(CHUNKS)]
-        se = [sb.tile([P, G, CW], F32, name="se%d" % c) for c in range(CHUNKS)]
+        pair = [sb.tile([P, G, 2 * CW], F32, name="pair%d" % c) for c in range(CHUNKS)]
+        pair_moved = [sb.tile([P, PACK, 2 * CW], F32, name="pair_moved%d" % c) for c in range(CHUNKS)]
 
-        def add_first(c):
+        def sums(c, early):
             nc.vector.tensor_tensor(out=part[c][:], in0=e[c][:, :, 0:CW], in1=e[c][:, :, CW : 2 * CW], op=ALU.add)
+            if early:
+                for g in range(G):
+                    nc.vector.tensor_scalar(
+                        out=pair[c][:, g, CW : 2 * CW], in0=th[c][:, g, :], scalar1=scale_of(g), scalar2=None, op0=ALU.mult
+                    )
+            nc.vector.tensor_tensor(out=pair[c][:, :, 0:CW], in0=part[c][:], in1=e[c][:, :, 2 * CW : 3 * CW], op=ALU.add)
+            if early:
+                for g in (0, 2, 1, 3):
+                    nc.sync.dma_start(out=pair_moved[c][ROWS * g : ROWS * (g + 1), :, :], in_=pair[c][:, g, :])
 
-        def add_second(c):
-            nc.vector.tensor_tensor(out=se[c][:], in0=part[c][:], in1=e[c][:, :, 2 * CW : 3 * CW], op=ALU.add)
-
-        w1_g = interleave("w1", w1_raw, True)
-        x0_g = interleave("x0", x_raw[0], False)
-        w1_q = quantize("w1", w1_g)
-        x0_q = quantize("x0", x0_g)
-        w2_g = interleave("w2", w2_raw, True)
+        w1_g = interleave("w1", w1_raw, CW, False)
+        x0_g = sb.tile([P, CW * PACK], BF16, name="x0_grp", align_bytes=64)
+        SPLIT = 88
+        nc.scalar.activation(out=word_order(x0_g[:, SPLIT * PACK :]), in_=row_order(x0_raw[:, :, SPLIT:]), func=ACT.Copy)
+        nc.vector.tensor_copy(out=word_order(x0_g[:, : SPLIT * PACK]), in_=row_order(x0_raw[:, :, :SPLIT]))
+        w1_q = quantize("w1", w1_g, CW)
+        x0_q = quantize("x0", x0_g, CW)
+        w2_g = interleave("w2", w2_raw, CW, True)
         for g in range(G):
-            product(banks[g][0][:, 0:CW], g, w1_q, x0_q)
-        w3_g = interleave("w3", w3_raw, False)
-        w2_q = quantize("w2", w2_g)
-        w3_q = quantize("w3", w3_g)
+            product(banks[g][0][:, 0:CW], g, w1_q, x0_q, 0)
+        w3_g = interleave("w3", w3_raw, CW, False)
+        w2_q = quantize("w2", w2_g, CW)
+        w3_q = quantize("w3", w3_g, CW)
+        x1_g = interleave("x1", x1_raw, CW, False)
+        nc.vector.transpose(out=hs_cols[:], in_=hs_rows[:])
+        x1_q = quantize("x1", x1_g, CW)
         w_q = [w1_q, w2_q, w3_q]
         for b in (1, 2):
             for g in range(G):
-                product(banks[g][1][:, (b - 1) * CW : b * CW], g, w_q[b], x0_q)
+                product(banks[g][1][:, (b - 1) * CW : b * CW], g, w_q[b], x0_q, 0)
         for g in range(G):
             nc.scalar.activation(out=th[0][:, g, :], in_=banks[g][0][:, 0:CW], func=ACT.Tanh)
             nc.scalar.activation(out=e[0][:, g, 0:CW], in_=banks[g][0][:, 0:CW], func=ACT.Exp)
         for g in range(G):
             nc.scalar.activation(out=e[0][:, g, CW : 3 * CW], in_=banks[g][1][:, 0 : 2 * CW], func=ACT.Exp)
 
-        def first_layer(c, x_q):
+        def first_layer(c, x_q, col0):
             s = (c + 1) % 2
             for b in range(3):
                 for g in range(G):
-                    product(banks[g][s][:, b * CW : (b + 1) * CW], g, w_q[b], x_q)
+                    product(banks[g][s][:, b * CW : (b + 1) * CW], g, w_q[b], x_q, col0)
             for g in range(G):
                 nc.scalar.activation(out=e[c][:, g, :], in_=banks[g][s][:, 0 : 3 * CW], func=ACT.Exp)
                 nc.scalar.activation(out=th[c][:, g, :], in_=banks[g][s][:, 0:CW], func=ACT.Tanh)
 
-        x1_g = interleave("x1", x_raw[1], False)
-        x1_q = quantize("x1", x1_g)
-        first_layer(1, x1_q)
-        x2_g = interleave("x2", x_raw[2], False)
-        x3_g = interleave("x3", x_raw[3], False)
-        x2_q = quantize("x2", x2_g)
-        x3_q = quantize("x3", x3_g)
-        add_first(0)
-        wo_g = interleave("wo", wo_raw, False)
-        add_second(0)
-        wo_q = quantize("wo", wo_g)
-        first_layer(2, x2_q)
-        add_first(1)
-        add_second(1)
-        first_layer(3, x3_q)
-        for c in (2, 3):
-            add_first(c)
-            add_second(c)
+        first_layer(1, x1_q, 0)
+        xl_g = interleave("xl", xl_raw, 2 * CW, False)
+        xl_q = quantize("xl", xl_g, 2 * CW)
+        sums(0, True)
+        LW = 2 * CW
+        e12l = sb.tile([P, G, 2 * LW], F32, name="e12l")
+        e3l = sb.tile([P, G, LW], F32, name="e3l")
+        thl = sb.tile([P, G, LW], F32, name="thl")
+        for b in range(2):
+            for q in range(2):
+                for g in reversed(range(G)):
+                    product(banks[g][1][:, b * LW + q * CW : b * LW + (q + 1) * CW], g, w_q[b], xl_q, q * CW)
+        for q in range(2):
+            for g in reversed(range(G)):
+                product(banks[g][0][:, q * CW : (q + 1) * CW], g, w3_q, xl_q, q * CW)
+        sums(1, True)
+        wo_g = interleave("wo", wo_raw, CW, False)
+        wo_q = quantize("wo", wo_g, CW)
+        for g in range(G):
+            nc.scalar.activation(out=e12l[:, g, :], in_=banks[g][1][:, :], func=ACT.Exp)
+            nc.scalar.activation(out=thl[:, g, :], in_=banks[g][1][:, 0:LW], func=ACT.Tanh)
+        for g in range(G):
+            nc.scalar.activation(out=e3l[:, g, :], in_=banks[g][0][:, 0:LW], func=ACT.Exp)
+        for q in range(2):
+            nc.vector.tensor_tensor(
+                out=part[2 + q][:], in0=e12l[:, :, q * CW : (q + 1) * CW], in1=e12l[:, :, LW + q * CW : LW + (q + 1) * CW], op=ALU.add
+            )
+        for q in range(2):
+            nc.vector.tensor_tensor(out=pair[2 + q][:, :, 0:CW], in0=part[2 + q][:], in1=e3l[:, :, q * CW : (q + 1) * CW], op=ALU.add)
 
         lse = [sb.tile([P, G, CW], F32, name="lse%d" % c) for c in range(CHUNKS)]
         hh = [sb.tile([P, G, CW], BF16, name="hh%d" % c) for c in range(CHUNKS)]
         moved = [sb.tile([P, PACK, CW], BF16, name="moved%d" % c) for c in range(CHUNKS)]
-        for c in range(CHUNKS):
-            for half in range(2):
-                gs = slice(2 * half, 2 * half + 2)
-                nc.scalar.activation(out=lse[c][:, gs, :], in_=se[c][:, gs, :], func=ACT.Ln)
+        words = [sb.tile([P, CW * PACK], BF16, name="words%d" % c, align_bytes=64) for c in range(CHUNKS)]
+        y = [sb.tile([P, G, 2 * CW], F32, name="y%d" % h) for h in range(2)]
+        outv = out.rearrange("g o n -> o g n")
+
+        def late_rows(c, step):
             for g in range(G):
+                if g % step == 0:
+                    nc.scalar.activation(out=lse[c][:, g : g + step, :], in_=pair[c][:, g : g + step, 0:CW], func=ACT.Ln)
                 nc.vector.scalar_tensor_tensor(
-                    out=hh[c][:, g, :], in0=th[c][:, g, :], scalar=hs_sb[:, g : g + 1], in1=lse[c][:, g, :],
+                    out=hh[c][:, g, :], in0=thl[:, g, (c - 2) * CW : (c - 1) * CW], scalar=scale_of(g), in1=lse[c][:, g, :],
                     op0=ALU.mult, op1=ALU.mult,
                 )
                 nc.sync.dma_start(out=moved[c][ROWS * g : ROWS * (g + 1), :, :], in_=hh[c][:, g, :])
 
-        outv = out.rearrange("g o n -> o g n")
+        def late_words(c):
+            nc.scalar.activation(out=word_order(words[c][:]), in_=row_order(moved[c][:]), func=ACT.Copy)
 
-        def second_product(c):
-            hh_g = interleave("hh%d" % c, moved[c], True)
-            hh_q = quantize("hh%d" % c, hh_g)
+        def early_ln(c):
+            nc.scalar.activation(out=lse[c][:], in_=pair_moved[c][:, :, 0:CW], func=ACT.Ln)
+
+        def early_words(c):
+            nc.vector.tensor_tensor(
+                out=word_order(words[c][:], 2), in0=row_order(lse[c][:], 2), in1=row_order(pair_moved[c][:, :, CW : 2 * CW], 2), op=ALU.mult
+            )
+
+        def second(c, s):
+            hh_q = quantize("hq%d" % c, words[c], CW)
             for g in range(G):
-                product(banks[g][c % 2][:, 0:CW], g, wo_q, hh_q)
+                product(banks[g][s][:, (c % 2) * CW : (c % 2 + 1) * CW], g, wo_q, hh_q, 0)
 
-        def finish(c):
-            cols = slice(c * CW, (c + 1) * CW)
-            y = sb.tile([P, G, CW], F32, name="y%d" % c)
-            for g in range(G):
-                nc.vector.tensor_tensor(out=y[:, g, :], in0=banks[g][c % 2][:, 0:CW], in1=res_sb[:, g, cols], op=ALU.add)
-                if g % 2 == 1:
-                    nc.sync.dma_start(out=outv[:, g - 1 : g + 1, cols], in_=y[:, g - 1 : g + 1, :])
+        def add(c0, nc_, s, g):
+            a, b = (c0 % 2) * CW, (c0 % 2 + nc_) * CW
+            nc.vector.tensor_tensor(
+                out=y[c0 // 2][:, g, a:b], in0=banks[g][s][:, a:b], in1=res_sb[:, g, c0 * CW : (c0 + nc_) * CW], op=ALU.add
+            )
 
-        second_product(0)
-        for c in range(CHUNKS):
-            if c + 1 < CHUNKS:
-                second_product(c + 1)
-            finish(c)
+        def store(c0, nc_, g0, ng):
+            a, b = (c0 % 2) * CW, (c0 % 2 + nc_) * CW
+            nc.sync.dma_start(out=outv[:, g0 : g0 + ng, c0 * CW : (c0 + nc_) * CW], in_=y[c0 // 2][:, g0 : g0 + ng, a:b])
+
+        late_rows(2, 1)
+        late_rows(3, 2)
+        early_ln(0)
+        early_words(0)
+        early_ln(1)
+        early_words(1)
+        second(0, 0)
+        second(1, 0)
+        late_words(2)
+        late_words(3)
+        for g in range(G):
+            if g == 0:
+                second(2, 1)
+            if g == 2:
+                second(3, 1)
+            add(0, 2, 0, g)
+            store(0, 2, g, 1)
+
+        for g in range(G):
+            add(2, 2, 1, g)
+            store(2, 2, g, 1)

from contextlib import ExitStack

import concourse.mybir as mybir

G, D, M, O, N = 4, 128, 128, 128, 512
FLOPS = 2 * G * D * M * N * 3 + 2 * G * M * O * N

F32 = mybir.dt.float32
BF16 = mybir.dt.bfloat16
U32 = mybir.dt.uint32
U8 = mybir.dt.uint8
FP8X4 = mybir.dt.float8_e4m3fn_x4
ACT = mybir.ActivationFunctionType
ALU = mybir.AluOpType

P = 128
PACK = 4
ROWS = 32
CW = 128
CHUNKS = N // CW
RUN = 4


def tile_rows_fsoftmaxthree_kernel(tc, x, w1, w2, w3, hs, wo2, res, out):
    nc = tc.nc
    with ExitStack() as ctx:
        sb = ctx.enter_context(tc.tile_pool(name="sb", bufs=1))
        ps = ctx.enter_context(tc.psum_pool(name="ps", bufs=1))
        ctx.enter_context(tc.manual_schedule())

        banks = [[ps.tile([P, 512], F32, name="bank%d_%d" % (g, s)) for s in range(2)] for g in range(G)]

        def load_packed(name, src, width):
            raw = sb.tile([P, PACK, width], F32, name=name + "_raw")
            nc.sync.dma_start(out=raw[:], in_=src)
            return raw

        def word_order(flat, run=RUN):
            return flat.rearrange("p (c i t) -> p c t i", i=run, t=PACK)

        def row_order(rows, run=RUN):
            return rows.rearrange("p t (c i) -> p c t i", i=run)

        def interleave(name, raw, width, on_scalar):
            grouped = sb.tile([P, width * PACK], BF16, name=name + "_grp", align_bytes=64)
            if on_scalar:
                nc.scalar.activation(out=word_order(grouped[:]), in_=row_order(raw[:]), func=ACT.Copy)
            else:
                nc.vector.tensor_copy(out=word_order(grouped[:]), in_=row_order(raw[:]))
            return grouped

        def quantize(name, grouped, width):
            codes = sb.tile([P, width], U32, name=name + "_codes", align_bytes=64)
            scales = sb.tile([P, width], U8, name=name + "_scales", align_bytes=64)
            nc.vector.quantize_mx(out=codes[:].bitcast(FP8X4), scales=scales[:], in_=grouped[:])
            return codes, scales

        def product(dst, g, stationary, moving, col0):
            rows = slice(ROWS * g, ROWS * (g + 1))
            cols = slice(col0, col0 + CW)
            nc.tensor.matmul_mx(
                out=dst,
                lhsT=stationary[0][rows, :].bitcast(FP8X4),
                lhsT_scale=stationary[1][rows, :],
                rhs=moving[0][rows, cols].bitcast(FP8X4),
                rhs_scale=moving[1][rows, cols],
                start=True,
                stop=True,
            )

        def packed_view(a):
            return a.rearrange("g (p j) c -> (g p) j c", j=PACK)

        xv = packed_view(x)
        hs_rows = sb.tile([P, ROWS], F32, name="hs_rows", align_bytes=64)
        hs_cols = sb.tile([P, ROWS], F32, name="hs_cols", align_bytes=64)
        nc.vector.memset(hs_rows[:], 0.0)
        w1_raw = load_packed("w1", packed_view(w1), CW)
        x0_raw = load_packed("x0", xv[:, :, 0:CW], CW)
        w2_raw = load_packed("w2", packed_view(w2), CW)
        w3_raw = load_packed("w3", packed_view(w3), CW)
        x1_raw = load_packed("x1", xv[:, :, CW : 2 * CW], CW)
        nc.sync.dma_start(out=hs_rows[0:P:8, :], in_=hs.rearrange("g (b c) o -> b g (c o)", c=ROWS))
        xl_raw = load_packed("xl", xv[:, :, 2 * CW : 4 * CW], 2 * CW)
        wo_raw = load_packed("wo", packed_view(wo2), CW)
        res_sb = sb.tile([P, G, N], F32, name="res_sb")
        nc.sync.dma_start(out=res_sb[:], in_=res.rearrange("g o n -> o g n"))

        def scale_of(g):
            return hs_cols[:, 8 * g : 8 * g + 1]

        e = [sb.tile([P, G, 3 * CW], F32, name="e%d" % c) for c in range(CHUNKS)]
        th = [sb.tile([P, G, CW], F32, name="th%d" % c) for c in range(CHUNKS)]
        part = [sb.tile([P, G, CW], F32, name="part%d" % c) for c in range(CHUNKS)]
        pair = [sb.tile([P, G, 2 * CW], F32, name="pair%d" % c) for c in range(CHUNKS)]
        pair_moved = [sb.tile([P, PACK, 2 * CW], F32, name="pair_moved%d" % c) for c in range(CHUNKS)]

        def sums(c, early):
            nc.vector.tensor_tensor(out=part[c][:], in0=e[c][:, :, 0:CW], in1=e[c][:, :, CW : 2 * CW], op=ALU.add)
            if early:
                for g in range(G):
                    nc.vector.tensor_scalar(
                        out=pair[c][:, g, CW : 2 * CW], in0=th[c][:, g, :], scalar1=scale_of(g), scalar2=None, op0=ALU.mult
                    )
            nc.vector.tensor_tensor(out=pair[c][:, :, 0:CW], in0=part[c][:], in1=e[c][:, :, 2 * CW : 3 * CW], op=ALU.add)
            if early:
                for g in (0, 2, 1, 3):
                    nc.sync.dma_start(out=pair_moved[c][ROWS * g : ROWS * (g + 1), :, :], in_=pair[c][:, g, :])

        w1_g = interleave("w1", w1_raw, CW, False)
        x0_g = sb.tile([P, CW * PACK], BF16, name="x0_grp", align_bytes=64)
        SPLIT = 88
        nc.scalar.activation(out=word_order(x0_g[:, SPLIT * PACK :]), in_=row_order(x0_raw[:, :, SPLIT:]), func=ACT.Copy)
        nc.vector.tensor_copy(out=word_order(x0_g[:, : SPLIT * PACK]), in_=row_order(x0_raw[:, :, :SPLIT]))
        w1_q = quantize("w1", w1_g, CW)
        x0_q = quantize("x0", x0_g, CW)
        w2_g = interleave("w2", w2_raw, CW, True)
        for g in range(G):
            product(banks[g][0][:, 0:CW], g, w1_q, x0_q, 0)
        w3_g = interleave("w3", w3_raw, CW, False)
        w2_q = quantize("w2", w2_g, CW)
        w3_q = quantize("w3", w3_g, CW)
        x1_g = interleave("x1", x1_raw, CW, False)
        nc.vector.transpose(out=hs_cols[:], in_=hs_rows[:])
        x1_q = quantize("x1", x1_g, CW)
        w_q = [w1_q, w2_q, w3_q]
        for b in (1, 2):
            for g in range(G):
                product(banks[g][1][:, (b - 1) * CW : b * CW], g, w_q[b], x0_q, 0)
        for g in range(G):
            nc.scalar.activation(out=th[0][:, g, :], in_=banks[g][0][:, 0:CW], func=ACT.Tanh)
            nc.scalar.activation(out=e[0][:, g, 0:CW], in_=banks[g][0][:, 0:CW], func=ACT.Exp)
        for g in range(G):
            nc.scalar.activation(out=e[0][:, g, CW : 3 * CW], in_=banks[g][1][:, 0 : 2 * CW], func=ACT.Exp)

        def first_layer(c, x_q, col0):
            s = (c + 1) % 2
            for b in range(3):
                for g in range(G):
                    product(banks[g][s][:, b * CW : (b + 1) * CW], g, w_q[b], x_q, col0)
            for g in range(G):
                nc.scalar.activation(out=e[c][:, g, :], in_=banks[g][s][:, 0 : 3 * CW], func=ACT.Exp)
                nc.scalar.activation(out=th[c][:, g, :], in_=banks[g][s][:, 0:CW], func=ACT.Tanh)

        first_layer(1, x1_q, 0)
        xl_g = interleave("xl", xl_raw, 2 * CW, False)
        xl_q = quantize("xl", xl_g, 2 * CW)
        sums(0, True)
        LW = 2 * CW
        e12l = sb.tile([P, G, 2 * LW], F32, name="e12l")
        e3l = sb.tile([P, G, LW], F32, name="e3l")
        thl = sb.tile([P, G, LW], F32, name="thl")
        for b in range(2):
            for q in range(2):
                for g in reversed(range(G)):
                    product(banks[g][1][:, b * LW + q * CW : b * LW + (q + 1) * CW], g, w_q[b], xl_q, q * CW)
        for q in range(2):
            for g in reversed(range(G)):
                product(banks[g][0][:, q * CW : (q + 1) * CW], g, w3_q, xl_q, q * CW)
        sums(1, True)
        wo_g = interleave("wo", wo_raw, CW, False)
        wo_q = quantize("wo", wo_g, CW)
        for g in range(G):
            nc.scalar.activation(out=e12l[:, g, :], in_=banks[g][1][:, :], func=ACT.Exp)
            nc.scalar.activation(out=thl[:, g, :], in_=banks[g][1][:, 0:LW], func=ACT.Tanh)
        for g in range(G):
            nc.scalar.activation(out=e3l[:, g, :], in_=banks[g][0][:, 0:LW], func=ACT.Exp)
        for q in range(2):
            nc.vector.tensor_tensor(
                out=part[2 + q][:], in0=e12l[:, :, q * CW : (q + 1) * CW], in1=e12l[:, :, LW + q * CW : LW + (q + 1) * CW], op=ALU.add
            )
        for q in range(2):
            nc.vector.tensor_tensor(out=pair[2 + q][:, :, 0:CW], in0=part[2 + q][:], in1=e3l[:, :, q * CW : (q + 1) * CW], op=ALU.add)

        lse = [sb.tile([P, G, CW], F32, name="lse%d" % c) for c in range(CHUNKS)]
        hh = [sb.tile([P, G, CW], BF16, name="hh%d" % c) for c in range(CHUNKS)]
        moved = [sb.tile([P, PACK, CW], BF16, name="moved%d" % c) for c in range(CHUNKS)]
        words = [sb.tile([P, CW * PACK], BF16, name="words%d" % c, align_bytes=64) for c in range(CHUNKS)]
        y = [sb.tile([P, G, 2 * CW], F32, name="y%d" % h) for h in range(2)]
        outv = out.rearrange("g o n -> o g n")

        def late_rows(c, step):
            for g in range(G):
                if g % step == 0:
                    nc.scalar.activation(out=lse[c][:, g : g + step, :], in_=pair[c][:, g : g + step, 0:CW], func=ACT.Ln)
                nc.vector.scalar_tensor_tensor(
                    out=hh[c][:, g, :], in0=thl[:, g, (c - 2) * CW : (c - 1) * CW], scalar=scale_of(g), in1=lse[c][:, g, :],
                    op0=ALU.mult, op1=ALU.mult,
                )
                nc.sync.dma_start(out=moved[c][ROWS * g : ROWS * (g + 1), :, :], in_=hh[c][:, g, :])

        def late_words(c):
            nc.scalar.activation(out=word_order(words[c][:]), in_=row_order(moved[c][:]), func=ACT.Copy)

        def early_ln(c):
            nc.scalar.activation(out=lse[c][:], in_=pair_moved[c][:, :, 0:CW], func=ACT.Ln)

        def early_words(c):
            nc.vector.tensor_tensor(
                out=word_order(words[c][:], 2), in0=row_order(lse[c][:], 2), in1=row_order(pair_moved[c][:, :, CW : 2 * CW], 2), op=ALU.mult
            )

        def second(c, s):
            hh_q = quantize("hq%d" % c, words[c], CW)
            for g in range(G):
                product(banks[g][s][:, (c % 2) * CW : (c % 2 + 1) * CW], g, wo_q, hh_q, 0)

        def add(c0, nc_, s, g):
            a, b = (c0 % 2) * CW, (c0 % 2 + nc_) * CW
            nc.vector.tensor_tensor(
                out=y[c0 // 2][:, g, a:b], in0=banks[g][s][:, a:b], in1=res_sb[:, g, c0 * CW : (c0 + nc_) * CW], op=ALU.add
            )

        def store(c0, nc_, g0, ng):
            a, b = (c0 % 2) * CW, (c0 % 2 + nc_) * CW
            nc.sync.dma_start(out=outv[:, g0 : g0 + ng, c0 * CW : (c0 + nc_) * CW], in_=y[c0 // 2][:, g0 : g0 + ng, a:b])

        late_rows(2, 1)
        late_rows(3, 2)
        early_ln(0)
        early_words(0)
        early_ln(1)
        early_words(1)
        second(0, 0)
        second(1, 0)
        late_words(2)
        late_words(3)
        for g in range(G):
            if g == 0:
                second(2, 1)
            if g == 2:
                second(3, 1)
            add(0, 2, 0, g)
            store(0, 2, g, 1)

        for g in range(G):
            add(2, 2, 1, g)
            store(2, 2, g, 1)
